import numpy as np
import ml_dtypes


def mxq(x, axis, fmt="e4m3"):
    dtype, down = {"e4m3": (ml_dtypes.float8_e4m3fn, 7), "e5m2": (ml_dtypes.float8_e5m2, 14)}[fmt]
    v = np.moveaxis(np.asarray(x, np.float32).astype(ml_dtypes.bfloat16).astype(np.float64), axis, -1)
    blocks = v.reshape(v.shape[:-1] + (-1, 32))
    amax = np.abs(blocks).max(-1, keepdims=True)
    byte = np.maximum(np.where(amax > 0, np.frexp(amax)[1] - 1 + 127, 0) - down, 1)
    scale = np.exp2(byte - 127.0)
    codes = (blocks / scale).astype(np.float32).astype(dtype).astype(np.float64)
    return np.moveaxis((codes * scale).reshape(v.shape), -1, axis)


WIDE = False


def mx_kscale(k):
    if not WIDE:
        return np.ones(k)
    levels = np.array([10, -10, 5, -5, 0])
    if k % 512:
        return np.exp2(np.random.permutation(np.resize(levels, k // 32))).repeat(32)
    a = np.empty((k // 512, 16))
    for p in range(k // 512):
        a[p, :8] = np.random.permutation(np.resize(levels, 8))
        for g in range(8):
            far = levels[np.abs(levels - a[p, g]) >= 10]
            a[p, g + 8] = far[np.random.randint(len(far))]
    return np.exp2(a.ravel()).repeat(32)


BF16 = ml_dtypes.bfloat16


def bf(x):
    return np.asarray(x, np.float32).astype(BF16)


def f64(x):
    return np.asarray(x).astype(np.float64)


E2M1 = np.array([0.0, 0.5, 1.0, 1.5, 2.0, 3.0, 4.0, 6.0, -0.0, -0.5, -1.0, -1.5, -2.0, -3.0, -4.0, -6.0])


def pack_weight(w, fmt):
    k, n = w.shape
    w = f64(bf(w)).reshape(k // 32, 32, n)
    amax = np.abs(w).max(1)
    if fmt == "e4m3":
        byte = np.frexp(amax)[1] - 1 + 127 - 7
    else:
        mant, ex = np.frexp(amax / 6.0)
        byte = np.where(mant > 0.5, ex, ex - 1) + 127
    byte = np.clip(np.where(amax > 0, byte, 1), 1, 254)
    scaled = (w * np.exp2(127.0 - byte)[:, None, :]).reshape(k, n).astype(np.float32)
    by_word = np.ascontiguousarray(scaled.reshape(k // 512, 128, 4, n).transpose(0, 1, 3, 2))
    if fmt == "e4m3":
        words = by_word.astype(ml_dtypes.float8_e4m3fn).view(np.uint8)
    else:
        c = by_word.astype(ml_dtypes.float4_e2m1fn).view(np.uint8) & 0xF
        words = c[..., 0::2] | (c[..., 1::2] << 4)
    return np.ascontiguousarray(words), np.ascontiguousarray(byte.astype(np.uint8).reshape(k // 512, 16, n))


def unpack_weight(words, scales, fmt):
    g, p, n, _ = words.shape
    if fmt == "e4m3":
        vals = np.ascontiguousarray(words).view(ml_dtypes.float8_e4m3fn).astype(np.float64)
    else:
        nib = np.empty((g, p, n, 4), np.uint8)
        nib[..., 0::2] = words & 0xF
        nib[..., 1::2] = words >> 4
        vals = E2M1[nib]
    vals = vals * np.repeat(np.exp2(scales.astype(np.float64) - 127.0), 8, axis=1)[..., None]
    return vals.transpose(0, 1, 3, 2).reshape(g * 512, n)
def pack4(w):
    words, scales = pack_weight(w, "e2m1")
    return words.reshape(words.shape[0], 128, -1), scales


def unpack4(words, scales):
    return unpack_weight(words.reshape(words.shape[0], 128, -1, 2), scales, "e2m1")


E, M, D, C, T = 4, 1024, 1024, 512, 512

LOCALITY = 1.5
SPREAD = 0.5


def setup_inputs():
    s, t = mx_kscale(E * D), mx_kscale(E * C)
    x = np.random.standard_normal((E, M, D)) * s.reshape(E, 1, D)
    points = LOCALITY * np.random.standard_normal((E * D, C)) / np.sqrt(D) / s[:, None]
    ratio = np.exp(SPREAD * np.random.standard_normal((E, C))) * t.reshape(E, C)
    scores = np.random.uniform(0.0, 1.0, (E * C, T))
    thresholds = np.random.uniform(0.25, 0.85, (1, T))
    thresholds[:, -1] = np.inf
    below = np.where(scores <= thresholds, 1.0, -1.0) / C / t[:, None]
    points_words, points_scales = pack4(points)
    below_words, below_scales = pack4(below)
    return {"x": bf(x), "points_words": points_words, "points_scales": points_scales,
            "ratio": bf(ratio), "below_words": below_words, "below_scales": below_scales}


def reference(x, points_words, points_scales, ratio, below_words, below_scales):
    points = unpack4(points_words, points_scales).reshape(E, D, C)
    below = unpack4(below_words, below_scales).reshape(E, C, T)
    z = mxq(f64(x), 2, "e4m3") @ points
    w = np.exp(z) * f64(ratio)[:, None, :]
    mass = mxq(w, 2, "e4m3") @ below
    return mass / mass[:, :, -1:]

@@ -1,0 +1,273 @@
+import math
+from contextlib import ExitStack
+
+import concourse.mybir as mybir
+from concourse.masks import make_identity
+
+E, M, D, C, T = 4, 1024, 1024, 512, 512
+FLOPS = 2 * E * M * C * (D + T)
+
+F32 = mybir.dt.float32
+BF16 = mybir.dt.bfloat16
+I32 = mybir.dt.int32
+U32 = mybir.dt.uint32
+U8 = mybir.dt.uint8
+FP8X4 = mybir.dt.float8_e4m3fn_x4
+FP4X4 = mybir.dt.float4_e2m1fn_x4
+ACT = mybir.ActivationFunctionType
+ALU = mybir.AluOpType
+
+P = 128
+ROWS = 512
+SUBS = ROWS // P
+STEPS = E * M // ROWS
+G = D // 512
+
+
+def tile_localised_signed_calibration_mass_s14_kernel(
+    tc, x, points_words, points_scales, ratio, below_words, below_scales, out
+):
+    nc = tc.nc
+    with ExitStack() as ctx:
+        keep = ctx.enter_context(tc.tile_pool(name="keep", bufs=1))
+        xin = ctx.enter_context(tc.tile_pool(name="xin", bufs=2 * STEPS))
+        strat = ctx.enter_context(tc.tile_pool(name="strat", bufs=E))
+        work = ctx.enter_context(tc.tile_pool(name="work", bufs=3))
+        outs = ctx.enter_context(tc.tile_pool(name="outs", bufs=3))
+        psum = ctx.enter_context(tc.psum_pool(name="psum", bufs=8))
+        ctx.enter_context(tc.manual_schedule())
+
+        x_tiles = {}
+        p_raw = {}
+
+        def load_x(step, half):
+            e, h = divmod(step, 2)
+            t = xin.tile([P, 2, D], BF16, name="xt", align_bytes=64)
+            rows = x[e].rearrange("(p q) k -> p q k", q=8)
+            q0 = 4 * h + 2 * half
+            nc.sync.dma_start(out=t[:], in_=rows[:, q0 : q0 + 2, :])
+            x_tiles[step, half] = t
+
+        def load_p(e):
+            t = strat.tile([P, G, 2 * C], U8, name="praw", align_bytes=64)
+            nc.sync.dma_start(
+                out=t[:].bitcast(I32),
+                in_=points_words[G * e : G * (e + 1)].bitcast(I32).rearrange("g p n -> p g n"),
+            )
+            p_raw[e] = t
+
+        rat = keep.tile([P, E, 4], BF16, name="rat")
+        nc.scalar.dma_start(out=rat[:], in_=ratio.rearrange("e (p t) -> p e t", t=4))
+
+        ps_raw = keep.tile([P, E * G, C], U8, name="psraw", align_bytes=64)
+        v_scales = keep.tile([P, E, T], U8, name="vscales", align_bytes=64)
+        v_words = keep.tile([P, E, 2 * T], U8, name="vwords", align_bytes=64)
+        nc.vector.memset(ps_raw[:].rearrange("p g n -> p (g n)").bitcast(I32), 0)
+        nc.gpsimd.memset(v_scales[:].rearrange("p e n -> p (e n)").bitcast(I32), 0)
+        ident = keep.tile([P, P], F32, name="ident")
+        make_identity(nc, ident[:])
+
+        load_x(0, 0)
+        load_p(0)
+        load_x(0, 1)
+        for q in range(4):
+            nc.scalar.dma_start(
+                out=ps_raw[32 * q : 32 * q + 4].bitcast(I32),
+                in_=points_scales[:, 4 * q : 4 * q + 4, :].bitcast(I32).rearrange("g r n -> r g n"),
+            )
+        load_x(1, 0)
+        load_x(1, 1)
+        nc.sync.dma_start(
+            out=v_words[:].bitcast(I32), in_=below_words.bitcast(I32).rearrange("e p n -> p e n")
+        )
+        for q in range(4):
+            nc.sync.dma_start(
+                out=v_scales[32 * q : 32 * q + 4].bitcast(I32),
+                in_=below_scales[:, 4 * q : 4 * q + 4, :].bitcast(I32).rearrange("e r n -> r e n"),
+            )
+        for e in range(1, E):
+            load_p(e)
+            for h in range(2):
+                load_x(2 * e + h, 0)
+                load_x(2 * e + h, 1)
+
+        rat32 = keep.tile([P, E * 4], F32, name="rat32")
+        expo = keep.tile([P, E * 4], I32, name="expo")
+        expo32 = keep.tile([P, E * 4], F32, name="expo32")
+        mant = keep.tile([P, E * 4], I32, name="mant")
+        ln_mant = keep.tile([P, E * 4], F32, name="lnmant")
+        ln_ratio = keep.tile([P, E * 4], F32, name="lnratio")
+        nc.vector.tensor_copy(out=rat32[:], in_=rat[:].rearrange("p e t -> p (e t)"))
+        bits = rat32[:].bitcast(I32)
+        nc.vector.tensor_scalar(
+            out=mant[:], in0=bits, scalar1=0x007FFFFF, scalar2=0x3F800000, op0=ALU.bitwise_and, op1=ALU.bitwise_or
+        )
+        nc.vector.tensor_scalar(
+            out=expo[:], in0=bits, scalar1=23, scalar2=255, op0=ALU.logical_shift_right, op1=ALU.bitwise_and
+        )
+        nc.scalar.activation(out=ln_mant[:], in_=mant[:].bitcast(F32), func=ACT.Ln)
+        nc.vector.tensor_scalar(out=expo32[:], in0=expo[:], scalar1=-127.0, scalar2=None, op0=ALU.add)
+        nc.vector.scalar_tensor_tensor(
+            out=ln_ratio[:], in0=expo32[:], scalar=math.log(2.0), in1=ln_mant[:], op0=ALU.mult, op1=ALU.add
+        )
+        warm = keep.tile([P, 1], F32, name="warm")
+        nc.scalar.activation(out=warm[:], in_=ln_ratio[:, 0:1], func=ACT.Exp)
+
+        p_words = {}
+        p_scales = {}
+
+        def permute_words(e):
+            t = strat.tile([P, G, 2 * C], U8, name="pwords", align_bytes=64)
+            for g in range(G):
+                nc.vector.tensor_copy(
+                    out=t[:, g, :].rearrange("p (t m b) -> p t m b", t=4, b=2),
+                    in_=p_raw[e][:, g, :].rearrange("p (m t b) -> p t m b", t=4, b=2),
+                )
+            p_words[e] = t
+
+        def permute_scales(e):
+            t = strat.tile([P, G, C], U8, name="pscales", align_bytes=64)
+            nc.vector.tensor_copy(
+                out=t[:].rearrange("p g (t m) -> p g t m", t=4),
+                in_=ps_raw[:, G * e : G * (e + 1), :].rearrange("p g (m t) -> p g t m", t=4),
+            )
+            p_scales[e] = t
+
+        tb = {}
+        xg = {}
+        xc = {}
+        zb = {}
+        wt = {}
+        wq = {}
+        ob = {}
+
+        def transposes(s):
+            for half in range(2):
+                words = x_tiles[s, half][:].rearrange("p q k -> p (q k)").bitcast(F32)
+                for g in range(G):
+                    bank = psum.tile([P, 2, 2, P], F32, name="bank")
+                    for q in range(2):
+                        for u in range(2):
+                            k0 = 512 * q + 256 * g
+                            nc.tensor.transpose(bank[:, q, u, :], words[:, k0 + u : k0 + 256 : 2], ident[:])
+                    tb[s, half, g] = bank
+
+        def copy_x(s):
+            t = work.tile([P, G, ROWS, 4], BF16, name="xg", align_bytes=64)
+            for half in range(2):
+                for g in range(G):
+                    nc.scalar.copy(
+                        out=t[:, g, 256 * half : 256 * (half + 1), :]
+                        .bitcast(F32)
+                        .rearrange("p (q r) u -> p q r u", q=2),
+                        in_=tb[s, half, g][:].rearrange("p q u r -> p q r u"),
+                    )
+            xg[s] = t
+
+        def quantize_x(s):
+            codes = work.tile([P, G, ROWS], U32, name="xcodes", align_bytes=64)
+            scales = work.tile([P, G, ROWS], U8, name="xscales", align_bytes=64)
+            for g in range(G):
+                nc.vector.quantize_mx(
+                    out=codes[:, g, :].bitcast(FP8X4),
+                    scales=scales[:, g, :],
+                    in_=xg[s][:, g].rearrange("p r t -> p (r t)"),
+                )
+            xc[s] = (codes, scales)
+
+        def first_matmul(s):
+            e = s // 2
+            codes, scales = xc[s]
+            for j in range(4):
+                bank = psum.tile([P, ROWS], F32, name="bank")
+                for g in range(G):
+                    nc.tensor.matmul_mx(
+                        out=bank[:],
+                        lhsT=p_words[e][:, g, 256 * j : 256 * (j + 1)].bitcast(FP4X4),
+                        lhsT_scale=p_scales[e][:, g, P * j : P * (j + 1)],
+                        rhs=codes[:, g, :].bitcast(FP8X4),
+                        rhs_scale=scales[:, g, :],
+                        start=(g == 0),
+                        stop=(g == G - 1),
+                    )
+                zb[s, j] = bank
+
+        def exp_z(s):
+            e = s // 2
+            t = work.tile([P, 4, ROWS], BF16, name="wt", align_bytes=64)
+            for j in range(4):
+                nc.scalar.activation(
+                    out=t[:, j, :], in_=zb[s, j][:], func=ACT.Exp, bias=ln_ratio[:, 4 * e + j : 4 * e + j + 1]
+                )
+            wt[s] = t
+
+        def quantize_w(s):
+            grouped = work.tile([P, ROWS, 4], BF16, name="wg", align_bytes=64)
+            codes = work.tile([P, ROWS], U32, name="wcodes", align_bytes=64)
+            scales = work.tile([P, ROWS], U8, name="wscales", align_bytes=64)
+            for c in range(2):
+                cols = slice(256 * c, 256 * (c + 1))
+                nc.vector.tensor_copy(out=grouped[:, cols, :], in_=wt[s][:, :, cols].rearrange("p t n -> p n t"))
+            for c in range(2):
+                cols = slice(256 * c, 256 * (c + 1))
+                nc.vector.quantize_mx(
+                    out=codes[:, cols].bitcast(FP8X4),
+                    scales=scales[:, cols],
+                    in_=grouped[:, cols, :].rearrange("p n t -> p (n t)"),
+                )
+            wq[s] = (codes, scales)
+
+        def second_matmul(s):
+            e = s // 2
+            codes, scales = wq[s]
+            for q in range(SUBS):
+                bank = psum.tile([P, T], F32, name="bank")
+                nc.tensor.matmul_mx(
+                    out=bank[:],
+                    lhsT=codes[:, P * q : P * (q + 1)].bitcast(FP8X4),
+                    lhsT_scale=scales[:, P * q : P * (q + 1)],
+                    rhs=v_words[:, e, :].bitcast(FP4X4),
+                    rhs_scale=v_scales[:, e, :],
+                    start=True,
+                    stop=True,
+                )
+                ob[s, q] = bank
+
+        def normalise(s):
+            e, h = divmod(s, 2)
+            rows = out[e].rearrange("(p q) c -> p q c", q=8)
+            o = outs.tile([P, SUBS, T], F32, name="o", align_bytes=64)
+            rec = []
+            for q in range(SUBS):
+                r = work.tile([P, 1], F32, name="rec%d" % q)
+                nc.vector.reciprocal(out=r[:], in_=ob[s, q][:, T - 1 : T])
+                rec.append(r)
+                if q == 1 or q == 3:
+                    v, a = (0, 1) if q == 1 else (2, 3)
+                    nc.vector.tensor_scalar(
+                        out=o[:, v, :], in0=ob[s, v][:], scalar1=rec[v][:], scalar2=None, op0=ALU.mult
+                    )
+                    nc.scalar.activation(out=o[:, a, :], in_=ob[s, a][:], func=ACT.Copy, scale=rec[a][:])
+                    q0 = 4 * h + v
+                    nc.sync.dma_start(out=rows[:, q0 : q0 + 2, :], in_=o[:, v : v + 2, :])
+
+        permute_words(0)
+        permute_scales(0)
+        for it in range(-2, STEPS):
+            t, a, b = it + 2, it + 1, it
+            if t < STEPS:
+                transposes(t)
+                copy_x(t)
+                quantize_x(t)
+            if 0 <= a < STEPS:
+                first_matmul(a)
+                exp_z(a)
+            if b >= 0:
+                second_matmul(b)
+                normalise(b)
+            if 0 <= a < STEPS:
+                quantize_w(a)
+            if it % 2 and (it + 3) // 2 < E:
+                permute_words((it + 3) // 2)
+            if it % 2 == 0 and 1 <= (it + 2) // 2 < E:
+                permute_scales((it + 2) // 2)

@@ -18,10 +18,12 @@ ACT = mybir.ActivationFunctionType
 ALU = mybir.AluOpType
 
 P = 128
-ROWS = 512
-SUBS = ROWS // P
-STEPS = E * M // ROWS
 G = D // 512
+Q = M // P
+STEP_LIST = [(e, q0, 4) for e in range(E) for q0 in (0, 4)]
+STEP_LIST = STEP_LIST[:-1] + [(3, 4, 2), (3, 6, 2)]
+STEPS = len(STEP_LIST)
+TAIL = 1
 
 
 def tile_localised_signed_calibration_mass_s14_kernel(
@@ -30,7 +32,7 @@ def tile_localised_signed_calibration_mass_s14_kernel(
     nc = tc.nc
     with ExitStack() as ctx:
         keep = ctx.enter_context(tc.tile_pool(name="keep", bufs=1))
-        xin = ctx.enter_context(tc.tile_pool(name="xin", bufs=2 * STEPS))
+        xin = ctx.enter_context(tc.tile_pool(name="xin", bufs=E * Q // 2))
         strat = ctx.enter_context(tc.tile_pool(name="strat", bufs=E))
         work = ctx.enter_context(tc.tile_pool(name="work", bufs=3))
         outs = ctx.enter_context(tc.tile_pool(name="outs", bufs=3))
@@ -40,13 +42,11 @@ def tile_localised_signed_calibration_mass_s14_kernel(
         x_tiles = {}
         p_raw = {}
 
-        def load_x(step, half):
-            e, h = divmod(step, 2)
+        def load_x(e, q):
             t = xin.tile([P, 2, D], BF16, name="xt", align_bytes=64)
-            rows = x[e].rearrange("(p q) k -> p q k", q=8)
-            q0 = 4 * h + 2 * half
-            nc.sync.dma_start(out=t[:], in_=rows[:, q0 : q0 + 2, :])
-            x_tiles[step, half] = t
+            rows = x[e].rearrange("(p q) k -> p q k", q=Q)
+            nc.sync.dma_start(out=t[:], in_=rows[:, q : q + 2, :])
+            x_tiles[e, q] = t
 
         def load_p(e):
             t = strat.tile([P, G, 2 * C], U8, name="praw", align_bytes=64)
@@ -63,20 +63,20 @@ def tile_localised_signed_calibration_mass_s14_kernel(
         v_scales = keep.tile([P, E, T], U8, name="vscales", align_bytes=64)
         v_words = keep.tile([P, E, 2 * T], U8, name="vwords", align_bytes=64)
         nc.vector.memset(ps_raw[:].rearrange("p g n -> p (g n)").bitcast(I32), 0)
-        nc.gpsimd.memset(v_scales[:].rearrange("p e n -> p (e n)").bitcast(I32), 0)
         ident = keep.tile([P, P], F32, name="ident")
         make_identity(nc, ident[:])
+        nc.gpsimd.memset(v_scales[:].rearrange("p e n -> p (e n)").bitcast(I32), 0)
 
         load_x(0, 0)
+        load_x(0, 2)
+        load_x(0, 4)
         load_p(0)
-        load_x(0, 1)
         for q in range(4):
             nc.scalar.dma_start(
                 out=ps_raw[32 * q : 32 * q + 4].bitcast(I32),
                 in_=points_scales[:, 4 * q : 4 * q + 4, :].bitcast(I32).rearrange("g r n -> r g n"),
             )
-        load_x(1, 0)
-        load_x(1, 1)
+        load_x(0, 6)
         nc.sync.dma_start(
             out=v_words[:].bitcast(I32), in_=below_words.bitcast(I32).rearrange("e p n -> p e n")
         )
@@ -87,9 +87,8 @@ def tile_localised_signed_calibration_mass_s14_kernel(
             )
         for e in range(1, E):
             load_p(e)
-            for h in range(2):
-                load_x(2 * e + h, 0)
-                load_x(2 * e + h, 1)
+            for q in range(0, Q, 2):
+                load_x(e, q)
 
         rat32 = keep.tile([P, E * 4], F32, name="rat32")
         expo = keep.tile([P, E * 4], I32, name="expo")
@@ -142,31 +141,33 @@ def tile_localised_signed_calibration_mass_s14_kernel(
         ob = {}
 
         def transposes(s):
-            for half in range(2):
-                words = x_tiles[s, half][:].rearrange("p q k -> p (q k)").bitcast(F32)
+            e, q0, nq = STEP_LIST[s]
+            for q in range(q0, q0 + nq, 2):
+                words = x_tiles[e, q][:].rearrange("p q k -> p (q k)").bitcast(F32)
                 for g in range(G):
                     bank = psum.tile([P, 2, 2, P], F32, name="bank")
-                    for q in range(2):
+                    for b in range(2):
                         for u in range(2):
-                            k0 = 512 * q + 256 * g
-                            nc.tensor.transpose(bank[:, q, u, :], words[:, k0 + u : k0 + 256 : 2], ident[:])
-                    tb[s, half, g] = bank
+                            k0 = 512 * b + 256 * g
+                            nc.tensor.transpose(bank[:, b, u, :], words[:, k0 + u : k0 + 256 : 2], ident[:])
+                    tb[e, q, g] = bank
 
         def copy_x(s):
-            t = work.tile([P, G, ROWS, 4], BF16, name="xg", align_bytes=64)
-            for half in range(2):
+            e, q0, nq = STEP_LIST[s]
+            t = work.tile([P, G, nq * P, 4], BF16, name="xg%d" % nq, align_bytes=64)
+            for q in range(q0, q0 + nq, 2):
                 for g in range(G):
+                    r0 = (q - q0) * P
                     nc.scalar.copy(
-                        out=t[:, g, 256 * half : 256 * (half + 1), :]
-                        .bitcast(F32)
-                        .rearrange("p (q r) u -> p q r u", q=2),
-                        in_=tb[s, half, g][:].rearrange("p q u r -> p q r u"),
+                        out=t[:, g, r0 : r0 + 256, :].bitcast(F32).rearrange("p (q r) u -> p q r u", q=2),
+                        in_=tb[e, q, g][:].rearrange("p q u r -> p q r u"),
                     )
             xg[s] = t
 
         def quantize_x(s):
-            codes = work.tile([P, G, ROWS], U32, name="xcodes", align_bytes=64)
-            scales = work.tile([P, G, ROWS], U8, name="xscales", align_bytes=64)
+            e, q0, nq = STEP_LIST[s]
+            codes = work.tile([P, G, nq * P], U32, name="xcodes%d" % nq, align_bytes=64)
+            scales = work.tile([P, G, nq * P], U8, name="xscales%d" % nq, align_bytes=64)
             for g in range(G):
                 nc.vector.quantize_mx(
                     out=codes[:, g, :].bitcast(FP8X4),
@@ -176,25 +177,28 @@ def tile_localised_signed_calibration_mass_s14_kernel(
             xc[s] = (codes, scales)
 
         def first_matmul(s):
-            e = s // 2
+            e, q0, nq = STEP_LIST[s]
             codes, scales = xc[s]
             for j in range(4):
-                bank = psum.tile([P, ROWS], F32, name="bank")
-                for g in range(G):
-                    nc.tensor.matmul_mx(
-                        out=bank[:],
-                        lhsT=p_words[e][:, g, 256 * j : 256 * (j + 1)].bitcast(FP4X4),
-                        lhsT_scale=p_scales[e][:, g, P * j : P * (j + 1)],
-                        rhs=codes[:, g, :].bitcast(FP8X4),
-                        rhs_scale=scales[:, g, :],
-                        start=(g == 0),
-                        stop=(g == G - 1),
-                    )
+                bank = psum.tile([P, nq * P], F32, name="bank")
+                width = nq * P if nq == 4 else P
+                for c0 in range(0, nq * P, width):
+                    cols = slice(c0, c0 + width)
+                    for g in range(G):
+                        nc.tensor.matmul_mx(
+                            out=bank[:, cols],
+                            lhsT=p_words[e][:, g, 256 * j : 256 * (j + 1)].bitcast(FP4X4),
+                            lhsT_scale=p_scales[e][:, g, P * j : P * (j + 1)],
+                            rhs=codes[:, g, cols].bitcast(FP8X4),
+                            rhs_scale=scales[:, g, cols],
+                            start=(g == 0),
+                            stop=(g == G - 1),
+                        )
                 zb[s, j] = bank
 
         def exp_z(s):
-            e = s // 2
-            t = work.tile([P, 4, ROWS], BF16, name="wt", align_bytes=64)
+            e, q0, nq = STEP_LIST[s]
+            t = work.tile([P, 4, nq * P], BF16, name="wt%d" % nq, align_bytes=64)
             for j in range(4):
                 nc.scalar.activation(
                     out=t[:, j, :], in_=zb[s, j][:], func=ACT.Exp, bias=ln_ratio[:, 4 * e + j : 4 * e + j + 1]
@@ -202,14 +206,16 @@ def tile_localised_signed_calibration_mass_s14_kernel(
             wt[s] = t
 
         def quantize_w(s):
-            grouped = work.tile([P, ROWS, 4], BF16, name="wg", align_bytes=64)
-            codes = work.tile([P, ROWS], U32, name="wcodes", align_bytes=64)
-            scales = work.tile([P, ROWS], U8, name="wscales", align_bytes=64)
+            e, q0, nq = STEP_LIST[s]
+            grouped = work.tile([P, nq * P, 4], BF16, name="wg%d" % nq, align_bytes=64)
+            codes = work.tile([P, nq * P], U32, name="wcodes%d" % nq, align_bytes=64)
+            scales = work.tile([P, nq * P], U8, name="wscales%d" % nq, align_bytes=64)
+            half = nq * P // 2
             for c in range(2):
-                cols = slice(256 * c, 256 * (c + 1))
+                cols = slice(half * c, half * (c + 1))
                 nc.vector.tensor_copy(out=grouped[:, cols, :], in_=wt[s][:, :, cols].rearrange("p t n -> p n t"))
             for c in range(2):
-                cols = slice(256 * c, 256 * (c + 1))
+                cols = slice(half * c, half * (c + 1))
                 nc.vector.quantize_mx(
                     out=codes[:, cols].bitcast(FP8X4),
                     scales=scales[:, cols],
@@ -218,9 +224,9 @@ def tile_localised_signed_calibration_mass_s14_kernel(
             wq[s] = (codes, scales)
 
         def second_matmul(s):
-            e = s // 2
+            e, q0, nq = STEP_LIST[s]
             codes, scales = wq[s]
-            for q in range(SUBS):
+            for q in range(nq):
                 bank = psum.tile([P, T], F32, name="bank")
                 nc.tensor.matmul_mx(
                     out=bank[:],
@@ -234,22 +240,28 @@ def tile_localised_signed_calibration_mass_s14_kernel(
                 ob[s, q] = bank
 
         def normalise(s):
-            e, h = divmod(s, 2)
-            rows = out[e].rearrange("(p q) c -> p q c", q=8)
-            o = outs.tile([P, SUBS, T], F32, name="o", align_bytes=64)
+            e, q0, nq = STEP_LIST[s]
+            rows = out[e].rearrange("(p q) c -> p q c", q=Q)
+            o = outs.tile([P, nq, T], F32, name="o%d" % nq, align_bytes=64)
             rec = []
-            for q in range(SUBS):
+            for q in range(nq):
                 r = work.tile([P, 1], F32, name="rec%d" % q)
                 nc.vector.reciprocal(out=r[:], in_=ob[s, q][:, T - 1 : T])
                 rec.append(r)
-                if q == 1 or q == 3:
-                    v, a = (0, 1) if q == 1 else (2, 3)
-                    nc.vector.tensor_scalar(
-                        out=o[:, v, :], in0=ob[s, v][:], scalar1=rec[v][:], scalar2=None, op0=ALU.mult
-                    )
-                    nc.scalar.activation(out=o[:, a, :], in_=ob[s, a][:], func=ACT.Copy, scale=rec[a][:])
-                    q0 = 4 * h + v
-                    nc.sync.dma_start(out=rows[:, q0 : q0 + 2, :], in_=o[:, v : v + 2, :])
+            for q in range(0, nq, 2):
+                nc.vector.tensor_scalar(
+                    out=o[:, q, :], in0=ob[s, q][:], scalar1=rec[q][:], scalar2=None, op0=ALU.mult
+                )
+                nc.scalar.activation(out=o[:, q + 1, :], in_=ob[s, q + 1][:], func=ACT.Copy, scale=rec[q + 1][:])
+                if s < STEPS - 1:
+                    nc.sync.dma_start(out=rows[:, q0 + q : q0 + q + 2, :], in_=o[:, q : q + 2, :])
+                else:
+                    for b in (q, q + 1):
+                        nc.sync.dma_start(out=rows[:, q0 + b : q0 + b + 1, :], in_=o[:, b : b + 1, :])
+
+        first_step = {}
+        for s, (e, q0, nq) in reversed(list(enumerate(STEP_LIST))):
+            first_step[e] = s
 
         permute_words(0)
         permute_scales(0)
@@ -264,10 +276,14 @@ def tile_localised_signed_calibration_mass_s14_kernel(
                 exp_z(a)
             if b >= 0:
                 second_matmul(b)
-                normalise(b)
-            if 0 <= a < STEPS:
+            if a >= STEPS - TAIL and a < STEPS:
                 quantize_w(a)
-            if it % 2 and (it + 3) // 2 < E:
-                permute_words((it + 3) // 2)
-            if it % 2 == 0 and 1 <= (it + 2) // 2 < E:
-                permute_scales((it + 2) // 2)
+            if b >= 0:
+                normalise(b)
+            if 0 <= a < STEPS - TAIL:
+                quantize_w(a)
+            for e in range(1, E):
+                if t == first_step[e] - 2:
+                    permute_words(e)
+                if t == first_step[e] - 1:
+                    permute_scales(e)

@@ -20,10 +20,14 @@ ALU = mybir.AluOpType
 P = 128
 G = D // 512
 Q = M // P
-STEP_LIST = [(e, q0, 4) for e in range(E) for q0 in (0, 4)]
-STEP_LIST = STEP_LIST[:-1] + [(3, 4, 2), (3, 6, 2)]
+STEP_LIST = [(e, q0, 4) for e in range(E) for q0 in (0, 4)][:-1] + [(3, 4, 2), (3, 6, 2)]
 STEPS = len(STEP_LIST)
 TAIL = 1
+VC = 2
+V_OUT = {0: (), 1: (0,), 2: (0, 2), 3: (0, 2, 3), 4: (0, 1, 2, 3)}
+NV = [2 - s % 2 if q == 4 else 1 for s, (e, q0, q) in enumerate(STEP_LIST)]
+CV = [2, 2] + [0] * (STEPS - 2)
+LATE = [s < STEPS - 1 for s in range(STEPS)]
 
 
 def tile_localised_signed_calibration_mass_s14_kernel(
@@ -42,10 +46,12 @@ def tile_localised_signed_calibration_mass_s14_kernel(
         x_tiles = {}
         p_raw = {}
 
-        def load_x(e, q):
+        def load_x(e, q, pieces=1):
             t = xin.tile([P, 2, D], BF16, name="xt", align_bytes=64)
             rows = x[e].rearrange("(p q) k -> p q k", q=Q)
-            nc.sync.dma_start(out=t[:], in_=rows[:, q : q + 2, :])
+            n = 2 // pieces
+            for b in range(0, 2, n):
+                nc.sync.dma_start(out=t[:, b : b + n, :], in_=rows[:, q + b : q + b + n, :])
             x_tiles[e, q] = t
 
         def load_p(e):
@@ -56,27 +62,33 @@ def tile_localised_signed_calibration_mass_s14_kernel(
             )
             p_raw[e] = t
 
+        def load_p_scales(queue, e0, e1):
+            for q in range(4):
+                queue.dma_start(
+                    out=ps_raw[32 * q : 32 * q + 4, G * e0 : G * e1, :].bitcast(I32),
+                    in_=points_scales[G * e0 : G * e1, 4 * q : 4 * q + 4, :].bitcast(I32).rearrange("g r n -> r g n"),
+                )
+
         rat = keep.tile([P, E, 4], BF16, name="rat")
         nc.scalar.dma_start(out=rat[:], in_=ratio.rearrange("e (p t) -> p e t", t=4))
 
         ps_raw = keep.tile([P, E * G, C], U8, name="psraw", align_bytes=64)
         v_scales = keep.tile([P, E, T], U8, name="vscales", align_bytes=64)
         v_words = keep.tile([P, E, 2 * T], U8, name="vwords", align_bytes=64)
-        nc.vector.memset(ps_raw[:].rearrange("p g n -> p (g n)").bitcast(I32), 0)
+        nc.vector.memset(ps_raw[:, :G].rearrange("p g n -> p (g n)").bitcast(I32), 0)
+        nc.vector.memset(ps_raw[:, G:].rearrange("p g n -> p (g n)").bitcast(I32), 0)
+        nc.vector.memset(v_scales[:].rearrange("p e n -> p (e n)").bitcast(I32), 0)
         ident = keep.tile([P, P], F32, name="ident")
         make_identity(nc, ident[:])
-        nc.gpsimd.memset(v_scales[:].rearrange("p e n -> p (e n)").bitcast(I32), 0)
 
-        load_x(0, 0)
+        load_p_scales(nc.gpsimd, 0, 1)
+        load_x(0, 0, 2)
         load_x(0, 2)
-        load_x(0, 4)
         load_p(0)
-        for q in range(4):
-            nc.scalar.dma_start(
-                out=ps_raw[32 * q : 32 * q + 4].bitcast(I32),
-                in_=points_scales[:, 4 * q : 4 * q + 4, :].bitcast(I32).rearrange("g r n -> r g n"),
-            )
+        load_x(0, 4)
         load_x(0, 6)
+        load_x(1, 0)
+        load_x(1, 2)
         nc.sync.dma_start(
             out=v_words[:].bitcast(I32), in_=below_words.bitcast(I32).rearrange("e p n -> p e n")
         )
@@ -85,7 +97,11 @@ def tile_localised_signed_calibration_mass_s14_kernel(
                 out=v_scales[32 * q : 32 * q + 4].bitcast(I32),
                 in_=below_scales[:, 4 * q : 4 * q + 4, :].bitcast(I32).rearrange("e r n -> r e n"),
             )
-        for e in range(1, E):
+        load_p(1)
+        load_x(1, 4)
+        load_x(1, 6)
+        load_p_scales(nc.sync, 1, E)
+        for e in range(2, E):
             load_p(e)
             for q in range(0, Q, 2):
                 load_x(e, q)
@@ -110,7 +126,7 @@ def tile_localised_signed_calibration_mass_s14_kernel(
             out=ln_ratio[:], in0=expo32[:], scalar=math.log(2.0), in1=ln_mant[:], op0=ALU.mult, op1=ALU.add
         )
         warm = keep.tile([P, 1], F32, name="warm")
-        nc.scalar.activation(out=warm[:], in_=ln_ratio[:, 0:1], func=ACT.Exp)
+        nc.scalar.activation(out=warm[:], in_=ln_mant[:, 0:1], func=ACT.Exp)
 
         p_words = {}
         p_scales = {}
@@ -158,7 +174,8 @@ def tile_localised_signed_calibration_mass_s14_kernel(
             for q in range(q0, q0 + nq, 2):
                 for g in range(G):
                     r0 = (q - q0) * P
-                    nc.scalar.copy(
+                    copy = nc.vector.tensor_copy if q - q0 < CV[s] else nc.scalar.copy
+                    copy(
                         out=t[:, g, r0 : r0 + 256, :].bitcast(F32).rearrange("p (q r) u -> p q r u", q=2),
                         in_=tb[e, q, g][:].rearrange("p q u r -> p q r u"),
                     )
@@ -213,7 +230,8 @@ def tile_localised_signed_calibration_mass_s14_kernel(
             half = nq * P // 2
             for c in range(2):
                 cols = slice(half * c, half * (c + 1))
-                nc.vector.tensor_copy(out=grouped[:, cols, :], in_=wt[s][:, :, cols].rearrange("p t n -> p n t"))
+                src = wt[s][:, :, cols].rearrange("p t n -> p n t")
+                nc.vector.tensor_copy(out=grouped[:, cols, :], in_=src)
             for c in range(2):
                 cols = slice(half * c, half * (c + 1))
                 nc.vector.quantize_mx(
@@ -248,42 +266,46 @@ def tile_localised_signed_calibration_mass_s14_kernel(
                 r = work.tile([P, 1], F32, name="rec%d" % q)
                 nc.vector.reciprocal(out=r[:], in_=ob[s, q][:, T - 1 : T])
                 rec.append(r)
-            for q in range(0, nq, 2):
-                nc.vector.tensor_scalar(
-                    out=o[:, q, :], in0=ob[s, q][:], scalar1=rec[q][:], scalar2=None, op0=ALU.mult
-                )
-                nc.scalar.activation(out=o[:, q + 1, :], in_=ob[s, q + 1][:], func=ACT.Copy, scale=rec[q + 1][:])
-                if s < STEPS - 1:
-                    nc.sync.dma_start(out=rows[:, q0 + q : q0 + q + 2, :], in_=o[:, q : q + 2, :])
+            for q in range(nq):
+                if q in V_OUT[NV[s]]:
+                    nc.vector.tensor_scalar(
+                        out=o[:, q, :], in0=ob[s, q][:], scalar1=rec[q][:], scalar2=None, op0=ALU.mult
+                    )
                 else:
-                    for b in (q, q + 1):
-                        nc.sync.dma_start(out=rows[:, q0 + b : q0 + b + 1, :], in_=o[:, b : b + 1, :])
+                    nc.scalar.activation(out=o[:, q, :], in_=ob[s, q][:], func=ACT.Copy, scale=rec[q][:])
+                if s == STEPS - 1:
+                    nc.sync.dma_start(out=rows[:, q0 + q : q0 + q + 1, :], in_=o[:, q : q + 1, :])
+                elif q % 2:
+                    nc.sync.dma_start(out=rows[:, q0 + q - 1 : q0 + q + 1, :], in_=o[:, q - 1 : q + 1, :])
 
         first_step = {}
         for s, (e, q0, nq) in reversed(list(enumerate(STEP_LIST))):
             first_step[e] = s
 
-        permute_words(0)
-        permute_scales(0)
         for it in range(-2, STEPS):
             t, a, b = it + 2, it + 1, it
             if t < STEPS:
                 transposes(t)
                 copy_x(t)
+                if t == 0:
+                    permute_words(0)
+                e = STEP_LIST[t][0]
+                if t == first_step[e] and t > 0:
+                    permute_scales(e)
                 quantize_x(t)
+                if t == 0:
+                    permute_scales(0)
             if 0 <= a < STEPS:
                 first_matmul(a)
                 exp_z(a)
             if b >= 0:
                 second_matmul(b)
-            if a >= STEPS - TAIL and a < STEPS:
+            if 0 <= a < STEPS and not LATE[a]:
                 quantize_w(a)
             if b >= 0:
                 normalise(b)
-            if 0 <= a < STEPS - TAIL:
+            if 0 <= a < STEPS and LATE[a]:
                 quantize_w(a)
             for e in range(1, E):
-                if t == first_step[e] - 2:
-                    permute_words(e)
                 if t == first_step[e] - 1:
-                    permute_scales(e)
+                    permute_words(e)

@@ -20,14 +20,17 @@ ALU = mybir.AluOpType
 P = 128
 G = D // 512
 Q = M // P
-STEP_LIST = [(e, q0, 4) for e in range(E) for q0 in (0, 4)][:-1] + [(3, 4, 2), (3, 6, 2)]
+UNITS = 8
+STEP_LIST = [(0, 0, 256), (0, 256, 256), (1, 0, 512), (2, 0, 512), (3, 0, 512), (4, 0, 512), (5, 0, 512), (6, 0, 512), (7, 0, 256), (7, 256, 256)]
 STEPS = len(STEP_LIST)
 TAIL = 1
+SEQ = 'wsTTTqaqcaikTqcBqNTikqaTcwsBqNTiakqTcBqNTikqaTcwsBqNTiakqTcBqNTikqaTcwsBqNTiakqTcBqNiakcaicBNkiBkBNN'
+GI = [False, False, False, False, False, False, False, False, False, False]
 VC = 2
 V_OUT = {0: (), 1: (0,), 2: (0, 2), 3: (0, 2, 3), 4: (0, 1, 2, 3)}
-NV = [2 - s % 2 if q == 4 else 1 for s, (e, q0, q) in enumerate(STEP_LIST)]
-CV = [2, 2] + [0] * (STEPS - 2)
-LATE = [s < STEPS - 1 for s in range(STEPS)]
+NV = [1, 2, 1, 1, 1, 1, 1, 1, 1, 2]
+CV = [0, 0, 0, 1, 0, 0, 2, 0, 0, 0, 2, 0, 0, 0, 2, 0]
+LATE = [s < STEPS - TAIL for s in range(STEPS)]
 
 
 def tile_localised_signed_calibration_mass_s14_kernel(
@@ -70,7 +73,7 @@ def tile_localised_signed_calibration_mass_s14_kernel(
                 )
 
         rat = keep.tile([P, E, 4], BF16, name="rat")
-        nc.scalar.dma_start(out=rat[:], in_=ratio.rearrange("e (p t) -> p e t", t=4))
+        nc.gpsimd.dma_start(out=rat[:], in_=ratio.rearrange("e (p t) -> p e t", t=4))
 
         ps_raw = keep.tile([P, E * G, C], U8, name="psraw", align_bytes=64)
         v_scales = keep.tile([P, E, T], U8, name="vscales", align_bytes=64)
@@ -81,8 +84,8 @@ def tile_localised_signed_calibration_mass_s14_kernel(
         ident = keep.tile([P, P], F32, name="ident")
         make_identity(nc, ident[:])
 
-        load_p_scales(nc.gpsimd, 0, 1)
-        load_x(0, 0, 2)
+        load_p_scales(nc.scalar, 0, 1)
+        load_x(0, 0)
         load_x(0, 2)
         load_p(0)
         load_x(0, 4)
@@ -154,11 +157,12 @@ def tile_localised_signed_calibration_mass_s14_kernel(
         zb = {}
         wt = {}
         wq = {}
+        wg = {}
         ob = {}
 
-        def transposes(s):
-            e, q0, nq = STEP_LIST[s]
-            for q in range(q0, q0 + nq, 2):
+        def transposes(n, halves):
+            e, q0 = n // 2, 4 * (n % 2)
+            for q in [q0 + h for h in halves]:
                 words = x_tiles[e, q][:].rearrange("p q k -> p (q k)").bitcast(F32)
                 for g in range(G):
                     bank = psum.tile([P, 2, 2, P], F32, name="bank")
@@ -166,74 +170,80 @@ def tile_localised_signed_calibration_mass_s14_kernel(
                         for u in range(2):
                             k0 = 512 * b + 256 * g
                             nc.tensor.transpose(bank[:, b, u, :], words[:, k0 + u : k0 + 256 : 2], ident[:])
-                    tb[e, q, g] = bank
+                    tb[n, q - q0, g] = bank
 
-        def copy_x(s):
-            e, q0, nq = STEP_LIST[s]
-            t = work.tile([P, G, nq * P, 4], BF16, name="xg%d" % nq, align_bytes=64)
-            for q in range(q0, q0 + nq, 2):
-                for g in range(G):
-                    r0 = (q - q0) * P
-                    copy = nc.vector.tensor_copy if q - q0 < CV[s] else nc.scalar.copy
-                    copy(
-                        out=t[:, g, r0 : r0 + 256, :].bitcast(F32).rearrange("p (q r) u -> p q r u", q=2),
-                        in_=tb[e, q, g][:].rearrange("p q u r -> p q r u"),
-                    )
-            xg[s] = t
+        def copy_x(n, q):
+            t = work.tile([P, G, 256, 4], BF16, name="xg", bufs=6, align_bytes=64)
+            for g in range(G):
+                copy = nc.vector.tensor_copy if g < CV[2 * n + q // 2] else nc.scalar.copy
+                copy(
+                    out=t[:, g].bitcast(F32).rearrange("p (q r) u -> p q r u", q=2),
+                    in_=tb[n, q, g][:].rearrange("p q u r -> p q r u"),
+                )
+            xg[n, q] = t
 
-        def quantize_x(s):
-            e, q0, nq = STEP_LIST[s]
-            codes = work.tile([P, G, nq * P], U32, name="xcodes%d" % nq, align_bytes=64)
-            scales = work.tile([P, G, nq * P], U8, name="xscales%d" % nq, align_bytes=64)
+        def quantize_x(n, q):
+            if q == 0:
+                codes = work.tile([P, G, 512], U32, name="xcodes", bufs=4, align_bytes=64)
+                scales = work.tile([P, G, 512], U8, name="xscales", bufs=4, align_bytes=64)
+                xc[n] = (codes, scales)
+            codes, scales = xc[n]
+            cols = slice(P * q, P * (q + 2))
             for g in range(G):
                 nc.vector.quantize_mx(
-                    out=codes[:, g, :].bitcast(FP8X4),
-                    scales=scales[:, g, :],
-                    in_=xg[s][:, g].rearrange("p r t -> p (r t)"),
+                    out=codes[:, g, cols].bitcast(FP8X4),
+                    scales=scales[:, g, cols],
+                    in_=xg[n, q][:, g].rearrange("p r t -> p (r t)"),
                 )
-            xc[s] = (codes, scales)
 
-        def first_matmul(s):
-            e, q0, nq = STEP_LIST[s]
-            codes, scales = xc[s]
-            for j in range(4):
-                bank = psum.tile([P, nq * P], F32, name="bank")
-                width = nq * P if nq == 4 else P
-                for c0 in range(0, nq * P, width):
-                    cols = slice(c0, c0 + width)
+        def first_matmul(s, js=(0, 1, 2, 3)):
+            n, r0, rows = STEP_LIST[s]
+            e = n // 2
+            codes, scales = xc[n]
+            width = 512 if rows == 512 else P
+            for j in js:
+                bank = psum.tile([P, rows], F32, name="bank")
+                for c in range(0, rows, width):
                     for g in range(G):
                         nc.tensor.matmul_mx(
-                            out=bank[:, cols],
+                            out=bank[:, c : c + width],
                             lhsT=p_words[e][:, g, 256 * j : 256 * (j + 1)].bitcast(FP4X4),
                             lhsT_scale=p_scales[e][:, g, P * j : P * (j + 1)],
-                            rhs=codes[:, g, cols].bitcast(FP8X4),
-                            rhs_scale=scales[:, g, cols],
+                            rhs=codes[:, g, r0 + c : r0 + c + width].bitcast(FP8X4),
+                            rhs_scale=scales[:, g, r0 + c : r0 + c + width],
                             start=(g == 0),
                             stop=(g == G - 1),
                         )
                 zb[s, j] = bank
 
-        def exp_z(s):
-            e, q0, nq = STEP_LIST[s]
-            t = work.tile([P, 4, nq * P], BF16, name="wt%d" % nq, align_bytes=64)
-            for j in range(4):
-                nc.scalar.activation(
-                    out=t[:, j, :], in_=zb[s, j][:], func=ACT.Exp, bias=ln_ratio[:, 4 * e + j : 4 * e + j + 1]
+        def exp_z(s, js=(0, 1, 2, 3)):
+            n, r0, rows = STEP_LIST[s]
+            if 0 in js:
+                t = work.tile([P, 4, rows], BF16, name="wt%d" % rows, align_bytes=64)
+                wt[s] = t
+            t = wt[s]
+            for j in js:
+                c = 4 * (n // 2) + j
+                nc.scalar.activation(out=t[:, j, :], in_=zb[s, j][:], func=ACT.Exp, bias=ln_ratio[:, c : c + 1])
+
+        def interleave_w(s):
+            n, r0, rows = STEP_LIST[s]
+            grouped = work.tile([P, rows, 4], BF16, name="wg%d" % rows, align_bytes=64)
+            halves = [slice(0, rows // 2), slice(rows // 2, rows)]
+            for h, cols in enumerate(halves):
+                nc.vector.tensor_copy(
+                    out=grouped[:, cols, :].rearrange("p (c i) t -> p c t i", i=4),
+                    in_=wt[s][:, :, cols].rearrange("p t (c i) -> p c t i", i=4),
                 )
-            wt[s] = t
+            wg[s] = grouped
 
         def quantize_w(s):
-            e, q0, nq = STEP_LIST[s]
-            grouped = work.tile([P, nq * P, 4], BF16, name="wg%d" % nq, align_bytes=64)
-            codes = work.tile([P, nq * P], U32, name="wcodes%d" % nq, align_bytes=64)
-            scales = work.tile([P, nq * P], U8, name="wscales%d" % nq, align_bytes=64)
-            half = nq * P // 2
-            for c in range(2):
-                cols = slice(half * c, half * (c + 1))
-                src = wt[s][:, :, cols].rearrange("p t n -> p n t")
-                nc.vector.tensor_copy(out=grouped[:, cols, :], in_=src)
-            for c in range(2):
-                cols = slice(half * c, half * (c + 1))
+            n, r0, rows = STEP_LIST[s]
+            grouped = wg[s]
+            codes = work.tile([P, rows], U32, name="wcodes%d" % rows, align_bytes=64)
+            scales = work.tile([P, rows], U8, name="wscales%d" % rows, align_bytes=64)
+            halves = [slice(0, rows // 2), slice(rows // 2, rows)]
+            for cols in halves:
                 nc.vector.quantize_mx(
                     out=codes[:, cols].bitcast(FP8X4),
                     scales=scales[:, cols],
@@ -242,25 +252,27 @@ def tile_localised_signed_calibration_mass_s14_kernel(
             wq[s] = (codes, scales)
 
         def second_matmul(s):
-            e, q0, nq = STEP_LIST[s]
+            n, r0, rows = STEP_LIST[s]
             codes, scales = wq[s]
-            for q in range(nq):
+            for q in range(rows // P):
                 bank = psum.tile([P, T], F32, name="bank")
                 nc.tensor.matmul_mx(
                     out=bank[:],
                     lhsT=codes[:, P * q : P * (q + 1)].bitcast(FP8X4),
                     lhsT_scale=scales[:, P * q : P * (q + 1)],
-                    rhs=v_words[:, e, :].bitcast(FP4X4),
-                    rhs_scale=v_scales[:, e, :],
+                    rhs=v_words[:, n // 2, :].bitcast(FP4X4),
+                    rhs_scale=v_scales[:, n // 2, :],
                     start=True,
                     stop=True,
                 )
                 ob[s, q] = bank
 
         def normalise(s):
-            e, q0, nq = STEP_LIST[s]
-            rows = out[e].rearrange("(p q) c -> p q c", q=Q)
-            o = outs.tile([P, nq, T], F32, name="o%d" % nq, align_bytes=64)
+            n, r0, rows = STEP_LIST[s]
+            nq = rows // P
+            q0 = 4 * (n % 2) + r0 // P
+            dst = out[n // 2].rearrange("(p q) c -> p q c", q=Q)
+            o = outs.tile([P, nq, T], F32, name="o%d" % nq, bufs=2 if nq < 4 else 3, align_bytes=64)
             rec = []
             for q in range(nq):
                 r = work.tile([P, 1], F32, name="rec%d" % q)
@@ -274,38 +286,34 @@ def tile_localised_signed_calibration_mass_s14_kernel(
                 else:
                     nc.scalar.activation(out=o[:, q, :], in_=ob[s, q][:], func=ACT.Copy, scale=rec[q][:])
                 if s == STEPS - 1:
-                    nc.sync.dma_start(out=rows[:, q0 + q : q0 + q + 1, :], in_=o[:, q : q + 1, :])
+                    nc.sync.dma_start(out=dst[:, q0 + q : q0 + q + 1, :], in_=o[:, q : q + 1, :])
                 elif q % 2:
-                    nc.sync.dma_start(out=rows[:, q0 + q - 1 : q0 + q + 1, :], in_=o[:, q - 1 : q + 1, :])
+                    nc.sync.dma_start(out=dst[:, q0 + q - 1 : q0 + q + 1, :], in_=o[:, q - 1 : q + 1, :])
 
-        first_step = {}
-        for s, (e, q0, nq) in reversed(list(enumerate(STEP_LIST))):
-            first_step[e] = s
-
-        for it in range(-2, STEPS):
-            t, a, b = it + 2, it + 1, it
-            if t < STEPS:
-                transposes(t)
-                copy_x(t)
-                if t == 0:
-                    permute_words(0)
-                e = STEP_LIST[t][0]
-                if t == first_step[e] and t > 0:
-                    permute_scales(e)
-                quantize_x(t)
-                if t == 0:
-                    permute_scales(0)
-            if 0 <= a < STEPS:
-                first_matmul(a)
-                exp_z(a)
-            if b >= 0:
-                second_matmul(b)
-            if 0 <= a < STEPS and not LATE[a]:
-                quantize_w(a)
-            if b >= 0:
-                normalise(b)
-            if 0 <= a < STEPS and LATE[a]:
-                quantize_w(a)
-            for e in range(1, E):
-                if t == first_step[e] - 1:
-                    permute_words(e)
+        count = {c: 0 for c in "TqacikBNws"}
+        for c in SEQ:
+            k = count[c]
+            count[c] += 1
+            if c == "T":
+                transposes(k // 2, (2 * (k % 2),))
+                copy_x(k // 2, 2 * (k % 2))
+            elif c == "q":
+                quantize_x(k // 2, 2 * (k % 2))
+            elif c == "a":
+                first_matmul(k, (0, 1))
+                exp_z(k, (0, 1))
+            elif c == "c":
+                first_matmul(k, (2, 3))
+                exp_z(k, (2, 3))
+            elif c == "i":
+                interleave_w(k)
+            elif c == "k":
+                quantize_w(k)
+            elif c == "B":
+                second_matmul(k)
+            elif c == "N":
+                normalise(k)
+            elif c == "w":
+                permute_words(k)
+            elif c == "s":
+                permute_scales(k)

@@ -18,19 +18,25 @@ ACT = mybir.ActivationFunctionType
 ALU = mybir.AluOpType
 
 P = 128
-G = D // 512
+PACK = 4
+K_PASS = P * PACK
+G = D // K_PASS
 Q = M // P
-UNITS = 8
-STEP_LIST = [(0, 0, 256), (0, 256, 256), (1, 0, 512), (2, 0, 512), (3, 0, 512), (4, 0, 512), (5, 0, 512), (6, 0, 512), (7, 0, 256), (7, 256, 256)]
-STEPS = len(STEP_LIST)
-TAIL = 1
-SEQ = 'wsTTTqaqcaikTqcBqNTikqaTcwsBqNTiakqTcBqNTikqaTcwsBqNTiakqTcBqNTikqaTcwsBqNTiakqTcBqNiakcaicBNkiBkBNN'
-GI = [False, False, False, False, False, False, False, False, False, False]
-VC = 2
-V_OUT = {0: (), 1: (0,), 2: (0, 2), 3: (0, 2, 3), 4: (0, 1, 2, 3)}
-NV = [1, 2, 1, 1, 1, 1, 1, 1, 1, 2]
-CV = [0, 0, 0, 1, 0, 0, 2, 0, 0, 0, 2, 0, 0, 0, 2, 0]
-LATE = [s < STEPS - TAIL for s in range(STEPS)]
+UNIT = 4 * P
+HALF = 2 * P
+UNITS = E * M // UNIT
+
+STEPS = [(n, 0, UNIT) for n in range(UNITS - 1)] + [(UNITS - 1, 0, HALF), (UNITS - 1, HALF, HALF)]
+
+REORDERED_HALVES = [half for half in range(4, 2 * UNITS) if half % 4 in (1, 2)]
+
+HEAD = "wTTqsTqTacqq"
+BODY = "paikpwcTsTqTBNqiTakcBqqN"
+TAIL = "iackacBiNkikBNBN"
+ORDER = HEAD + BODY * 3 + TAIL
+
+X_BANKS_ON_VECTOR = [1, 0, 0, 1] + [0, 0, 0, 2] * 3
+OUT_BANKS_ON_VECTOR = [0, 2] * 3 + [1, 1, 0]
 
 
 def tile_localised_signed_calibration_mass_s14_kernel(
@@ -39,221 +45,226 @@ def tile_localised_signed_calibration_mass_s14_kernel(
     nc = tc.nc
     with ExitStack() as ctx:
         keep = ctx.enter_context(tc.tile_pool(name="keep", bufs=1))
-        xin = ctx.enter_context(tc.tile_pool(name="xin", bufs=E * Q // 2))
-        strat = ctx.enter_context(tc.tile_pool(name="strat", bufs=E))
+        x_pool = ctx.enter_context(tc.tile_pool(name="x_pool", bufs=E * Q // 2))
+        strata = ctx.enter_context(tc.tile_pool(name="strata", bufs=E))
         work = ctx.enter_context(tc.tile_pool(name="work", bufs=3))
-        outs = ctx.enter_context(tc.tile_pool(name="outs", bufs=3))
+        ahead = ctx.enter_context(tc.tile_pool(name="ahead", bufs=6))
+        codes_pool = ctx.enter_context(tc.tile_pool(name="codes_pool", bufs=4))
         psum = ctx.enter_context(tc.psum_pool(name="psum", bufs=8))
         ctx.enter_context(tc.manual_schedule())
 
-        x_tiles = {}
+        x_rows = {}
         p_raw = {}
 
-        def load_x(e, q, pieces=1):
-            t = xin.tile([P, 2, D], BF16, name="xt", align_bytes=64)
-            rows = x[e].rearrange("(p q) k -> p q k", q=Q)
-            n = 2 // pieces
-            for b in range(0, 2, n):
-                nc.sync.dma_start(out=t[:, b : b + n, :], in_=rows[:, q + b : q + b + n, :])
-            x_tiles[e, q] = t
+        def load_x(e, q):
+            t = x_pool.tile([P, 2, D], BF16, name="x_tile", align_bytes=64)
+            nc.sync.dma_start(out=t[:], in_=x[e].rearrange("(p q) k -> p q k", q=Q)[:, q : q + 2, :])
+            x_rows[e, q] = t
 
-        def load_p(e):
-            t = strat.tile([P, G, 2 * C], U8, name="praw", align_bytes=64)
-            nc.sync.dma_start(
-                out=t[:].bitcast(I32),
-                in_=points_words[G * e : G * (e + 1)].bitcast(I32).rearrange("g p n -> p g n"),
-            )
+        def load_p_words(e):
+            t = strata.tile([P, G, 2 * C], U8, name="p_raw_tile", align_bytes=64)
+            src = points_words[G * e : G * (e + 1)].bitcast(I32)
+            nc.sync.dma_start(out=t[:].bitcast(I32), in_=src.rearrange("g p n -> p g n"))
             p_raw[e] = t
 
-        def load_p_scales(queue, e0, e1):
-            for q in range(4):
+        def load_p_scales(queue, e0, e1, quadrants):
+            for i in quadrants:
+                src = points_scales[G * e0 : G * e1, 4 * i : 4 * i + 4, :].bitcast(I32)
                 queue.dma_start(
-                    out=ps_raw[32 * q : 32 * q + 4, G * e0 : G * e1, :].bitcast(I32),
-                    in_=points_scales[G * e0 : G * e1, 4 * q : 4 * q + 4, :].bitcast(I32).rearrange("g r n -> r g n"),
+                    out=p_scales_raw[32 * i : 32 * i + 4, G * e0 : G * e1, :].bitcast(I32),
+                    in_=src.rearrange("g r n -> r g n"),
                 )
 
-        rat = keep.tile([P, E, 4], BF16, name="rat")
-        nc.gpsimd.dma_start(out=rat[:], in_=ratio.rearrange("e (p t) -> p e t", t=4))
+        ratio_tile = keep.tile([P, E, PACK], BF16, name="ratio_tile")
+        nc.scalar.dma_start(out=ratio_tile[:], in_=ratio.rearrange("e (p t) -> p e t", t=PACK))
 
-        ps_raw = keep.tile([P, E * G, C], U8, name="psraw", align_bytes=64)
-        v_scales = keep.tile([P, E, T], U8, name="vscales", align_bytes=64)
-        v_words = keep.tile([P, E, 2 * T], U8, name="vwords", align_bytes=64)
-        nc.vector.memset(ps_raw[:, :G].rearrange("p g n -> p (g n)").bitcast(I32), 0)
-        nc.vector.memset(ps_raw[:, G:].rearrange("p g n -> p (g n)").bitcast(I32), 0)
+        p_scales_raw = keep.tile([P, E * G, C], U8, name="p_scales_raw", align_bytes=64)
+        v_scales = keep.tile([P, E, T], U8, name="v_scales", align_bytes=64)
+        v_words = keep.tile([P, E, 2 * T], U8, name="v_words", align_bytes=64)
+        nc.vector.memset(p_scales_raw[:, :G].rearrange("p g n -> p (g n)").bitcast(I32), 0)
+        nc.vector.memset(p_scales_raw[:, G:].rearrange("p g n -> p (g n)").bitcast(I32), 0)
         nc.vector.memset(v_scales[:].rearrange("p e n -> p (e n)").bitcast(I32), 0)
         ident = keep.tile([P, P], F32, name="ident")
         make_identity(nc, ident[:])
 
-        load_p_scales(nc.scalar, 0, 1)
+        load_p_scales(nc.scalar, 0, 1, (2, 3))
+        load_p_scales(nc.gpsimd, 0, 1, (0, 1))
         load_x(0, 0)
+        load_p_words(0)
         load_x(0, 2)
-        load_p(0)
         load_x(0, 4)
         load_x(0, 6)
         load_x(1, 0)
         load_x(1, 2)
-        nc.sync.dma_start(
-            out=v_words[:].bitcast(I32), in_=below_words.bitcast(I32).rearrange("e p n -> p e n")
-        )
-        for q in range(4):
+        nc.sync.dma_start(out=v_words[:].bitcast(I32), in_=below_words.bitcast(I32).rearrange("e p n -> p e n"))
+        for i in range(4):
             nc.sync.dma_start(
-                out=v_scales[32 * q : 32 * q + 4].bitcast(I32),
-                in_=below_scales[:, 4 * q : 4 * q + 4, :].bitcast(I32).rearrange("e r n -> r e n"),
+                out=v_scales[32 * i : 32 * i + 4].bitcast(I32),
+                in_=below_scales[:, 4 * i : 4 * i + 4, :].bitcast(I32).rearrange("e r n -> r e n"),
             )
-        load_p(1)
+        load_p_words(1)
         load_x(1, 4)
         load_x(1, 6)
-        load_p_scales(nc.sync, 1, E)
+        load_p_scales(nc.sync, 1, E, range(4))
         for e in range(2, E):
-            load_p(e)
+            load_p_words(e)
             for q in range(0, Q, 2):
                 load_x(e, q)
 
-        rat32 = keep.tile([P, E * 4], F32, name="rat32")
-        expo = keep.tile([P, E * 4], I32, name="expo")
-        expo32 = keep.tile([P, E * 4], F32, name="expo32")
-        mant = keep.tile([P, E * 4], I32, name="mant")
-        ln_mant = keep.tile([P, E * 4], F32, name="lnmant")
-        ln_ratio = keep.tile([P, E * 4], F32, name="lnratio")
-        nc.vector.tensor_copy(out=rat32[:], in_=rat[:].rearrange("p e t -> p (e t)"))
-        bits = rat32[:].bitcast(I32)
+        ratio32 = keep.tile([P, E * PACK], F32, name="ratio32")
+        mantissa = keep.tile([P, E * PACK], I32, name="mantissa")
+        exponent = keep.tile([P, E * PACK], I32, name="exponent")
+        exponent32 = keep.tile([P, E * PACK], F32, name="exponent32")
+        ln_mantissa = keep.tile([P, E * PACK], F32, name="ln_mantissa")
+        ln_ratio = keep.tile([P, E * PACK], F32, name="ln_ratio")
+        nc.vector.tensor_copy(out=ratio32[:], in_=ratio_tile[:].rearrange("p e t -> p (e t)"))
+        bits = ratio32[:].bitcast(I32)
         nc.vector.tensor_scalar(
-            out=mant[:], in0=bits, scalar1=0x007FFFFF, scalar2=0x3F800000, op0=ALU.bitwise_and, op1=ALU.bitwise_or
+            out=mantissa[:], in0=bits, scalar1=0x007FFFFF, scalar2=0x3F800000, op0=ALU.bitwise_and, op1=ALU.bitwise_or
         )
         nc.vector.tensor_scalar(
-            out=expo[:], in0=bits, scalar1=23, scalar2=255, op0=ALU.logical_shift_right, op1=ALU.bitwise_and
+            out=exponent[:], in0=bits, scalar1=23, scalar2=255, op0=ALU.logical_shift_right, op1=ALU.bitwise_and
         )
-        nc.scalar.activation(out=ln_mant[:], in_=mant[:].bitcast(F32), func=ACT.Ln)
-        nc.vector.tensor_scalar(out=expo32[:], in0=expo[:], scalar1=-127.0, scalar2=None, op0=ALU.add)
+        nc.scalar.activation(out=ln_mantissa[:], in_=mantissa[:].bitcast(F32), func=ACT.Ln)
+        nc.vector.tensor_scalar(out=exponent32[:], in0=exponent[:], scalar1=-127.0, scalar2=None, op0=ALU.add)
         nc.vector.scalar_tensor_tensor(
-            out=ln_ratio[:], in0=expo32[:], scalar=math.log(2.0), in1=ln_mant[:], op0=ALU.mult, op1=ALU.add
+            out=ln_ratio[:], in0=exponent32[:], scalar=math.log(2.0), in1=ln_mantissa[:], op0=ALU.mult, op1=ALU.add
         )
-        warm = keep.tile([P, 1], F32, name="warm")
-        nc.scalar.activation(out=warm[:], in_=ln_mant[:, 0:1], func=ACT.Exp)
+        table_load = keep.tile([P, 1], F32, name="table_load")
+        nc.scalar.activation(out=table_load[:], in_=ln_mantissa[:, 0:1], func=ACT.Exp)
 
         p_words = {}
         p_scales = {}
 
         def permute_words(e):
-            t = strat.tile([P, G, 2 * C], U8, name="pwords", align_bytes=64)
+            t = strata.tile([P, G, 2 * C], U8, name="p_words_tile", align_bytes=64)
             for g in range(G):
                 nc.vector.tensor_copy(
-                    out=t[:, g, :].rearrange("p (t m b) -> p t m b", t=4, b=2),
-                    in_=p_raw[e][:, g, :].rearrange("p (m t b) -> p t m b", t=4, b=2),
+                    out=t[:, g, :].rearrange("p (t m b) -> p t m b", t=PACK, b=2),
+                    in_=p_raw[e][:, g, :].rearrange("p (m t b) -> p t m b", t=PACK, b=2),
                 )
             p_words[e] = t
 
         def permute_scales(e):
-            t = strat.tile([P, G, C], U8, name="pscales", align_bytes=64)
+            t = strata.tile([P, G, C], U8, name="p_scales_tile", align_bytes=64)
             nc.vector.tensor_copy(
-                out=t[:].rearrange("p g (t m) -> p g t m", t=4),
-                in_=ps_raw[:, G * e : G * (e + 1), :].rearrange("p g (m t) -> p g t m", t=4),
+                out=t[:].rearrange("p g (t m) -> p g t m", t=PACK),
+                in_=p_scales_raw[:, G * e : G * (e + 1), :].rearrange("p g (m t) -> p g t m", t=PACK),
             )
             p_scales[e] = t
 
-        tb = {}
-        xg = {}
-        xc = {}
-        zb = {}
-        wt = {}
-        wq = {}
-        wg = {}
-        ob = {}
+        x_reordered = {}
+        x_grouped = {}
+        x_codes = {}
 
-        def transposes(n, halves):
-            e, q0 = n // 2, 4 * (n % 2)
-            for q in [q0 + h for h in halves]:
-                words = x_tiles[e, q][:].rearrange("p q k -> p (q k)").bitcast(F32)
-                for g in range(G):
-                    bank = psum.tile([P, 2, 2, P], F32, name="bank")
-                    for b in range(2):
-                        for u in range(2):
-                            k0 = 512 * b + 256 * g
-                            nc.tensor.transpose(bank[:, b, u, :], words[:, k0 + u : k0 + 256 : 2], ident[:])
-                    tb[n, q - q0, g] = bank
+        def words_of(half):
+            n, h = divmod(half, 2)
+            return x_rows[n // 2, 4 * (n % 2) + 2 * h][:].rearrange("p q k -> p (q k)").bitcast(F32)
 
-        def copy_x(n, q):
-            t = work.tile([P, G, 256, 4], BF16, name="xg", bufs=6, align_bytes=64)
+        def reorder_x(i):
+            half = REORDERED_HALVES[i]
+            t = work.tile([P, 2 * G, 2, P], F32, name="x_reordered_tile", align_bytes=64)
+            nc.vector.tensor_copy(out=t[:], in_=words_of(half).rearrange("p (a m u) -> p a u m", a=2 * G, u=2))
+            x_reordered[half] = t
+
+        def transpose_x(half):
+            banks = []
             for g in range(G):
-                copy = nc.vector.tensor_copy if g < CV[2 * n + q // 2] else nc.scalar.copy
+                bank = psum.tile([P, 2, 2, P], F32, name="bank")
+                for q in range(2):
+                    for u in range(2):
+                        if half in REORDERED_HALVES:
+                            words = x_reordered[half][:, G * q + g, u, :]
+                        else:
+                            k0 = D // 2 * q + K_PASS // 2 * g
+                            words = words_of(half)[:, k0 + u : k0 + K_PASS // 2 : 2]
+                        nc.tensor.transpose(bank[:, q, u, :], words, ident[:])
+                banks.append(bank)
+            t = ahead.tile([P, G, HALF, PACK], BF16, name="x_grouped_tile", align_bytes=64)
+            for g in range(G):
+                copy = nc.vector.tensor_copy if g < X_BANKS_ON_VECTOR[half] else nc.scalar.copy
                 copy(
                     out=t[:, g].bitcast(F32).rearrange("p (q r) u -> p q r u", q=2),
-                    in_=tb[n, q, g][:].rearrange("p q u r -> p q r u"),
+                    in_=banks[g][:].rearrange("p q u r -> p q r u"),
                 )
-            xg[n, q] = t
+            x_grouped[half] = t
 
-        def quantize_x(n, q):
-            if q == 0:
-                codes = work.tile([P, G, 512], U32, name="xcodes", bufs=4, align_bytes=64)
-                scales = work.tile([P, G, 512], U8, name="xscales", bufs=4, align_bytes=64)
-                xc[n] = (codes, scales)
-            codes, scales = xc[n]
-            cols = slice(P * q, P * (q + 2))
+        def quantise_x(half):
+            n, h = divmod(half, 2)
+            if h == 0:
+                codes = codes_pool.tile([P, G, UNIT], U32, name="x_codes_tile", align_bytes=64)
+                scales = codes_pool.tile([P, G, UNIT], U8, name="x_scales_tile", align_bytes=64)
+                x_codes[n] = (codes, scales)
+            codes, scales = x_codes[n]
+            cols = slice(HALF * h, HALF * (h + 1))
             for g in range(G):
                 nc.vector.quantize_mx(
                     out=codes[:, g, cols].bitcast(FP8X4),
                     scales=scales[:, g, cols],
-                    in_=xg[n, q][:, g].rearrange("p r t -> p (r t)"),
+                    in_=x_grouped[half][:, g].rearrange("p r t -> p (r t)"),
                 )
 
-        def first_matmul(s, js=(0, 1, 2, 3)):
-            n, r0, rows = STEP_LIST[s]
+        w_slots = {}
+        w_grouped = {}
+        w_codes = {}
+        out_banks = {}
+
+        def first_matmul(s, slots):
+            n, r0, rows = STEPS[s]
             e = n // 2
-            codes, scales = xc[n]
-            width = 512 if rows == 512 else P
-            for j in js:
+            codes, scales = x_codes[n]
+            if slots[0] == 0:
+                w_slots[s] = work.tile([P, PACK, rows], BF16, name="w_slots_%d" % rows, align_bytes=64)
+            width = UNIT if rows == UNIT else P
+            banks = []
+            for t in slots:
                 bank = psum.tile([P, rows], F32, name="bank")
                 for c in range(0, rows, width):
+                    cols = slice(r0 + c, r0 + c + width)
                     for g in range(G):
                         nc.tensor.matmul_mx(
                             out=bank[:, c : c + width],
-                            lhsT=p_words[e][:, g, 256 * j : 256 * (j + 1)].bitcast(FP4X4),
-                            lhsT_scale=p_scales[e][:, g, P * j : P * (j + 1)],
-                            rhs=codes[:, g, r0 + c : r0 + c + width].bitcast(FP8X4),
-                            rhs_scale=scales[:, g, r0 + c : r0 + c + width],
+                            lhsT=p_words[e][:, g, 2 * P * t : 2 * P * (t + 1)].bitcast(FP4X4),
+                            lhsT_scale=p_scales[e][:, g, P * t : P * (t + 1)],
+                            rhs=codes[:, g, cols].bitcast(FP8X4),
+                            rhs_scale=scales[:, g, cols],
                             start=(g == 0),
                             stop=(g == G - 1),
                         )
-                zb[s, j] = bank
+                banks.append(bank)
+            for t, bank in zip(slots, banks):
+                bias = ln_ratio[:, PACK * e + t : PACK * e + t + 1]
+                nc.scalar.activation(out=w_slots[s][:, t, :], in_=bank[:], func=ACT.Exp, bias=bias)
 
-        def exp_z(s, js=(0, 1, 2, 3)):
-            n, r0, rows = STEP_LIST[s]
-            if 0 in js:
-                t = work.tile([P, 4, rows], BF16, name="wt%d" % rows, align_bytes=64)
-                wt[s] = t
-            t = wt[s]
-            for j in js:
-                c = 4 * (n // 2) + j
-                nc.scalar.activation(out=t[:, j, :], in_=zb[s, j][:], func=ACT.Exp, bias=ln_ratio[:, c : c + 1])
+        def halves_of(rows):
+            return [slice(0, rows // 2), slice(rows // 2, rows)]
 
         def interleave_w(s):
-            n, r0, rows = STEP_LIST[s]
-            grouped = work.tile([P, rows, 4], BF16, name="wg%d" % rows, align_bytes=64)
-            halves = [slice(0, rows // 2), slice(rows // 2, rows)]
-            for h, cols in enumerate(halves):
+            rows = STEPS[s][2]
+            t = work.tile([P, rows, PACK], BF16, name="w_grouped_%d" % rows, align_bytes=64)
+            for cols in halves_of(rows):
                 nc.vector.tensor_copy(
-                    out=grouped[:, cols, :].rearrange("p (c i) t -> p c t i", i=4),
-                    in_=wt[s][:, :, cols].rearrange("p t (c i) -> p c t i", i=4),
+                    out=t[:, cols, :].rearrange("p (c i) t -> p c t i", i=4),
+                    in_=w_slots[s][:, :, cols].rearrange("p t (c i) -> p c t i", i=4),
                 )
-            wg[s] = grouped
+            w_grouped[s] = t
 
-        def quantize_w(s):
-            n, r0, rows = STEP_LIST[s]
-            grouped = wg[s]
-            codes = work.tile([P, rows], U32, name="wcodes%d" % rows, align_bytes=64)
-            scales = work.tile([P, rows], U8, name="wscales%d" % rows, align_bytes=64)
-            halves = [slice(0, rows // 2), slice(rows // 2, rows)]
-            for cols in halves:
+        def quantise_w(s):
+            rows = STEPS[s][2]
+            codes = work.tile([P, rows], U32, name="w_codes_%d" % rows, align_bytes=64)
+            scales = work.tile([P, rows], U8, name="w_scales_%d" % rows, align_bytes=64)
+            for cols in halves_of(rows):
                 nc.vector.quantize_mx(
                     out=codes[:, cols].bitcast(FP8X4),
                     scales=scales[:, cols],
-                    in_=grouped[:, cols, :].rearrange("p n t -> p (n t)"),
+                    in_=w_grouped[s][:, cols, :].rearrange("p n t -> p (n t)"),
                 )
-            wq[s] = (codes, scales)
+            w_codes[s] = (codes, scales)
 
         def second_matmul(s):
-            n, r0, rows = STEP_LIST[s]
-            codes, scales = wq[s]
+            n, r0, rows = STEPS[s]
+            codes, scales = w_codes[s]
+            out_banks[s] = []
             for q in range(rows // P):
                 bank = psum.tile([P, T], F32, name="bank")
                 nc.tensor.matmul_mx(
@@ -265,55 +276,48 @@ def tile_localised_signed_calibration_mass_s14_kernel(
                     start=True,
                     stop=True,
                 )
-                ob[s, q] = bank
+                out_banks[s].append(bank)
 
         def normalise(s):
-            n, r0, rows = STEP_LIST[s]
-            nq = rows // P
+            n, r0, rows = STEPS[s]
+            blocks = rows // P
             q0 = 4 * (n % 2) + r0 // P
             dst = out[n // 2].rearrange("(p q) c -> p q c", q=Q)
-            o = outs.tile([P, nq, T], F32, name="o%d" % nq, bufs=2 if nq < 4 else 3, align_bytes=64)
-            rec = []
-            for q in range(nq):
-                r = work.tile([P, 1], F32, name="rec%d" % q)
-                nc.vector.reciprocal(out=r[:], in_=ob[s, q][:, T - 1 : T])
-                rec.append(r)
-            for q in range(nq):
-                if q in V_OUT[NV[s]]:
+            result = work.tile([P, blocks, T], F32, name="result_%d" % blocks, align_bytes=64)
+            inverse = []
+            for q in range(blocks):
+                t = work.tile([P, 1], F32, name="inverse_%d" % q)
+                nc.vector.reciprocal(out=t[:], in_=out_banks[s][q][:, T - 1 : T])
+                inverse.append(t)
+            on_vector = (0, 2, 1, 3)[: OUT_BANKS_ON_VECTOR[s]] if blocks == 4 else range(OUT_BANKS_ON_VECTOR[s])
+            for q in range(blocks):
+                if q in on_vector:
                     nc.vector.tensor_scalar(
-                        out=o[:, q, :], in0=ob[s, q][:], scalar1=rec[q][:], scalar2=None, op0=ALU.mult
+                        out=result[:, q, :], in0=out_banks[s][q][:], scalar1=inverse[q][:], scalar2=None, op0=ALU.mult
                     )
                 else:
-                    nc.scalar.activation(out=o[:, q, :], in_=ob[s, q][:], func=ACT.Copy, scale=rec[q][:])
-                if s == STEPS - 1:
-                    nc.sync.dma_start(out=dst[:, q0 + q : q0 + q + 1, :], in_=o[:, q : q + 1, :])
+                    nc.scalar.activation(
+                        out=result[:, q, :], in_=out_banks[s][q][:], func=ACT.Copy, scale=inverse[q][:]
+                    )
+                if s == len(STEPS) - 1:
+                    nc.sync.dma_start(out=dst[:, q0 + q : q0 + q + 1, :], in_=result[:, q : q + 1, :])
                 elif q % 2:
-                    nc.sync.dma_start(out=dst[:, q0 + q - 1 : q0 + q + 1, :], in_=o[:, q - 1 : q + 1, :])
+                    nc.sync.dma_start(out=dst[:, q0 + q - 1 : q0 + q + 1, :], in_=result[:, q - 1 : q + 1, :])
 
-        count = {c: 0 for c in "TqacikBNws"}
-        for c in SEQ:
-            k = count[c]
-            count[c] += 1
-            if c == "T":
-                transposes(k // 2, (2 * (k % 2),))
-                copy_x(k // 2, 2 * (k % 2))
-            elif c == "q":
-                quantize_x(k // 2, 2 * (k % 2))
-            elif c == "a":
-                first_matmul(k, (0, 1))
-                exp_z(k, (0, 1))
-            elif c == "c":
-                first_matmul(k, (2, 3))
-                exp_z(k, (2, 3))
-            elif c == "i":
-                interleave_w(k)
-            elif c == "k":
-                quantize_w(k)
-            elif c == "B":
-                second_matmul(k)
-            elif c == "N":
-                normalise(k)
-            elif c == "w":
-                permute_words(k)
-            elif c == "s":
-                permute_scales(k)
+        stages = {
+            "p": reorder_x,
+            "T": transpose_x,
+            "q": quantise_x,
+            "a": lambda s: first_matmul(s, (0, 1)),
+            "c": lambda s: first_matmul(s, (2, 3)),
+            "i": interleave_w,
+            "k": quantise_w,
+            "B": second_matmul,
+            "N": normalise,
+            "w": permute_words,
+            "s": permute_scales,
+        }
+        done = {letter: 0 for letter in stages}
+        for letter in ORDER:
+            stages[letter](done[letter])
+            done[letter] += 1

import math
from contextlib import ExitStack

import concourse.mybir as mybir
from concourse.masks import make_identity

E, M, D, C, T = 4, 1024, 1024, 512, 512
FLOPS = 2 * E * M * C * (D + T)

F32 = mybir.dt.float32
BF16 = mybir.dt.bfloat16
I32 = mybir.dt.int32
U32 = mybir.dt.uint32
U8 = mybir.dt.uint8
FP8X4 = mybir.dt.float8_e4m3fn_x4
FP4X4 = mybir.dt.float4_e2m1fn_x4
ACT = mybir.ActivationFunctionType
ALU = mybir.AluOpType

P = 128
PACK = 4
K_PASS = P * PACK
G = D // K_PASS
Q = M // P
UNIT = 4 * P
HALF = 2 * P
UNITS = E * M // UNIT

STEPS = [(n, 0, UNIT) for n in range(UNITS - 1)] + [(UNITS - 1, 0, HALF), (UNITS - 1, HALF, HALF)]

REORDERED_HALVES = [half for half in range(4, 2 * UNITS) if half % 4 in (1, 2)]

HEAD = "wTTqsTqTacqq"
BODY = "paikpwcTsTqTBNqiTakcBqqN"
TAIL = "iackacBiNkikBNBN"
ORDER = HEAD + BODY * 3 + TAIL

X_BANKS_ON_VECTOR = [1, 0, 0, 1] + [0, 0, 0, 2] * 3
OUT_BANKS_ON_VECTOR = [0, 2] * 3 + [1, 1, 0]


def tile_localised_signed_calibration_mass_s14_kernel(
    tc, x, points_words, points_scales, ratio, below_words, below_scales, out
):
    nc = tc.nc
    with ExitStack() as ctx:
        keep = ctx.enter_context(tc.tile_pool(name="keep", bufs=1))
        x_pool = ctx.enter_context(tc.tile_pool(name="x_pool", bufs=E * Q // 2))
        strata = ctx.enter_context(tc.tile_pool(name="strata", bufs=E))
        work = ctx.enter_context(tc.tile_pool(name="work", bufs=3))
        ahead = ctx.enter_context(tc.tile_pool(name="ahead", bufs=6))
        codes_pool = ctx.enter_context(tc.tile_pool(name="codes_pool", bufs=4))
        psum = ctx.enter_context(tc.psum_pool(name="psum", bufs=8))
        ctx.enter_context(tc.manual_schedule())

        x_rows = {}
        p_raw = {}

        def load_x(e, q):
            t = x_pool.tile([P, 2, D], BF16, name="x_tile", align_bytes=64)
            nc.sync.dma_start(out=t[:], in_=x[e].rearrange("(p q) k -> p q k", q=Q)[:, q : q + 2, :])
            x_rows[e, q] = t

        def load_p_words(e):
            t = strata.tile([P, G, 2 * C], U8, name="p_raw_tile", align_bytes=64)
            src = points_words[G * e : G * (e + 1)].bitcast(I32)
            nc.sync.dma_start(out=t[:].bitcast(I32), in_=src.rearrange("g p n -> p g n"))
            p_raw[e] = t

        def load_p_scales(queue, e0, e1, quadrants):
            for i in quadrants:
                src = points_scales[G * e0 : G * e1, 4 * i : 4 * i + 4, :].bitcast(I32)
                queue.dma_start(
                    out=p_scales_raw[32 * i : 32 * i + 4, G * e0 : G * e1, :].bitcast(I32),
                    in_=src.rearrange("g r n -> r g n"),
                )

        ratio_tile = keep.tile([P, E, PACK], BF16, name="ratio_tile")
        nc.scalar.dma_start(out=ratio_tile[:], in_=ratio.rearrange("e (p t) -> p e t", t=PACK))

        p_scales_raw = keep.tile([P, E * G, C], U8, name="p_scales_raw", align_bytes=64)
        v_scales = keep.tile([P, E, T], U8, name="v_scales", align_bytes=64)
        v_words = keep.tile([P, E, 2 * T], U8, name="v_words", align_bytes=64)
        nc.vector.memset(p_scales_raw[:, :G].rearrange("p g n -> p (g n)").bitcast(I32), 0)
        nc.vector.memset(p_scales_raw[:, G:].rearrange("p g n -> p (g n)").bitcast(I32), 0)
        nc.vector.memset(v_scales[:].rearrange("p e n -> p (e n)").bitcast(I32), 0)
        ident = keep.tile([P, P], F32, name="ident")
        make_identity(nc, ident[:])

        load_p_scales(nc.scalar, 0, 1, (2, 3))
        load_p_scales(nc.gpsimd, 0, 1, (0, 1))
        load_x(0, 0)
        load_p_words(0)
        load_x(0, 2)
        load_x(0, 4)
        load_x(0, 6)
        load_x(1, 0)
        load_x(1, 2)
        nc.sync.dma_start(out=v_words[:].bitcast(I32), in_=below_words.bitcast(I32).rearrange("e p n -> p e n"))
        for i in range(4):
            nc.sync.dma_start(
                out=v_scales[32 * i : 32 * i + 4].bitcast(I32),
                in_=below_scales[:, 4 * i : 4 * i + 4, :].bitcast(I32).rearrange("e r n -> r e n"),
            )
        load_p_words(1)
        load_x(1, 4)
        load_x(1, 6)
        load_p_scales(nc.sync, 1, E, range(4))
        for e in range(2, E):
            load_p_words(e)
            for q in range(0, Q, 2):
                load_x(e, q)

        ratio32 = keep.tile([P, E * PACK], F32, name="ratio32")
        mantissa = keep.tile([P, E * PACK], I32, name="mantissa")
        exponent = keep.tile([P, E * PACK], I32, name="exponent")
        exponent32 = keep.tile([P, E * PACK], F32, name="exponent32")
        ln_mantissa = keep.tile([P, E * PACK], F32, name="ln_mantissa")
        ln_ratio = keep.tile([P, E * PACK], F32, name="ln_ratio")
        nc.vector.tensor_copy(out=ratio32[:], in_=ratio_tile[:].rearrange("p e t -> p (e t)"))
        bits = ratio32[:].bitcast(I32)
        nc.vector.tensor_scalar(
            out=mantissa[:], in0=bits, scalar1=0x007FFFFF, scalar2=0x3F800000, op0=ALU.bitwise_and, op1=ALU.bitwise_or
        )
        nc.vector.tensor_scalar(
            out=exponent[:], in0=bits, scalar1=23, scalar2=255, op0=ALU.logical_shift_right, op1=ALU.bitwise_and
        )
        nc.scalar.activation(out=ln_mantissa[:], in_=mantissa[:].bitcast(F32), func=ACT.Ln)
        nc.vector.tensor_scalar(out=exponent32[:], in0=exponent[:], scalar1=-127.0, scalar2=None, op0=ALU.add)
        nc.vector.scalar_tensor_tensor(
            out=ln_ratio[:], in0=exponent32[:], scalar=math.log(2.0), in1=ln_mantissa[:], op0=ALU.mult, op1=ALU.add
        )
        table_load = keep.tile([P, 1], F32, name="table_load")
        nc.scalar.activation(out=table_load[:], in_=ln_mantissa[:, 0:1], func=ACT.Exp)

        p_words = {}
        p_scales = {}

        def permute_words(e):
            t = strata.tile([P, G, 2 * C], U8, name="p_words_tile", align_bytes=64)
            for g in range(G):
                nc.vector.tensor_copy(
                    out=t[:, g, :].rearrange("p (t m b) -> p t m b", t=PACK, b=2),
                    in_=p_raw[e][:, g, :].rearrange("p (m t b) -> p t m b", t=PACK, b=2),
                )
            p_words[e] = t

        def permute_scales(e):
            t = strata.tile([P, G, C], U8, name="p_scales_tile", align_bytes=64)
            nc.vector.tensor_copy(
                out=t[:].rearrange("p g (t m) -> p g t m", t=PACK),
                in_=p_scales_raw[:, G * e : G * (e + 1), :].rearrange("p g (m t) -> p g t m", t=PACK),
            )
            p_scales[e] = t

        x_reordered = {}
        x_grouped = {}
        x_codes = {}

        def words_of(half):
            n, h = divmod(half, 2)
            return x_rows[n // 2, 4 * (n % 2) + 2 * h][:].rearrange("p q k -> p (q k)").bitcast(F32)

        def reorder_x(i):
            half = REORDERED_HALVES[i]
            t = work.tile([P, 2 * G, 2, P], F32, name="x_reordered_tile", align_bytes=64)
            nc.vector.tensor_copy(out=t[:], in_=words_of(half).rearrange("p (a m u) -> p a u m", a=2 * G, u=2))
            x_reordered[half] = t

        def transpose_x(half):
            banks = []
            for g in range(G):
                bank = psum.tile([P, 2, 2, P], F32, name="bank")
                for q in range(2):
                    for u in range(2):
                        if half in REORDERED_HALVES:
                            words = x_reordered[half][:, G * q + g, u, :]
                        else:
                            k0 = D // 2 * q + K_PASS // 2 * g
                            words = words_of(half)[:, k0 + u : k0 + K_PASS // 2 : 2]
                        nc.tensor.transpose(bank[:, q, u, :], words, ident[:])
                banks.append(bank)
            t = ahead.tile([P, G, HALF, PACK], BF16, name="x_grouped_tile", align_bytes=64)
            for g in range(G):
                copy = nc.vector.tensor_copy if g < X_BANKS_ON_VECTOR[half] else nc.scalar.copy
                copy(
                    out=t[:, g].bitcast(F32).rearrange("p (q r) u -> p q r u", q=2),
                    in_=banks[g][:].rearrange("p q u r -> p q r u"),
                )
            x_grouped[half] = t

        def quantise_x(half):
            n, h = divmod(half, 2)
            if h == 0:
                codes = codes_pool.tile([P, G, UNIT], U32, name="x_codes_tile", align_bytes=64)
                scales = codes_pool.tile([P, G, UNIT], U8, name="x_scales_tile", align_bytes=64)
                x_codes[n] = (codes, scales)
            codes, scales = x_codes[n]
            cols = slice(HALF * h, HALF * (h + 1))
            for g in range(G):
                nc.vector.quantize_mx(
                    out=codes[:, g, cols].bitcast(FP8X4),
                    scales=scales[:, g, cols],
                    in_=x_grouped[half][:, g].rearrange("p r t -> p (r t)"),
                )

        w_slots = {}
        w_grouped = {}
        w_codes = {}
        out_banks = {}

        def first_matmul(s, slots):
            n, r0, rows = STEPS[s]
            e = n // 2
            codes, scales = x_codes[n]
            if slots[0] == 0:
                w_slots[s] = work.tile([P, PACK, rows], BF16, name="w_slots_%d" % rows, align_bytes=64)
            width = UNIT if rows == UNIT else P
            banks = []
            for t in slots:
                bank = psum.tile([P, rows], F32, name="bank")
                for c in range(0, rows, width):
                    cols = slice(r0 + c, r0 + c + width)
                    for g in range(G):
                        nc.tensor.matmul_mx(
                            out=bank[:, c : c + width],
                            lhsT=p_words[e][:, g, 2 * P * t : 2 * P * (t + 1)].bitcast(FP4X4),
                            lhsT_scale=p_scales[e][:, g, P * t : P * (t + 1)],
                            rhs=codes[:, g, cols].bitcast(FP8X4),
                            rhs_scale=scales[:, g, cols],
                            start=(g == 0),
                            stop=(g == G - 1),
                        )
                banks.append(bank)
            for t, bank in zip(slots, banks):
                bias = ln_ratio[:, PACK * e + t : PACK * e + t + 1]
                nc.scalar.activation(out=w_slots[s][:, t, :], in_=bank[:], func=ACT.Exp, bias=bias)

        def halves_of(rows):
            return [slice(0, rows // 2), slice(rows // 2, rows)]

        def interleave_w(s):
            rows = STEPS[s][2]
            t = work.tile([P, rows, PACK], BF16, name="w_grouped_%d" % rows, align_bytes=64)
            for cols in halves_of(rows):
                nc.vector.tensor_copy(
                    out=t[:, cols, :].rearrange("p (c i) t -> p c t i", i=4),
                    in_=w_slots[s][:, :, cols].rearrange("p t (c i) -> p c t i", i=4),
                )
            w_grouped[s] = t

        def quantise_w(s):
            rows = STEPS[s][2]
            codes = work.tile([P, rows], U32, name="w_codes_%d" % rows, align_bytes=64)
            scales = work.tile([P, rows], U8, name="w_scales_%d" % rows, align_bytes=64)
            for cols in halves_of(rows):
                nc.vector.quantize_mx(
                    out=codes[:, cols].bitcast(FP8X4),
                    scales=scales[:, cols],
                    in_=w_grouped[s][:, cols, :].rearrange("p n t -> p (n t)"),
                )
            w_codes[s] = (codes, scales)

        def second_matmul(s):
            n, r0, rows = STEPS[s]
            codes, scales = w_codes[s]
            out_banks[s] = []
            for q in range(rows // P):
                bank = psum.tile([P, T], F32, name="bank")
                nc.tensor.matmul_mx(
                    out=bank[:],
                    lhsT=codes[:, P * q : P * (q + 1)].bitcast(FP8X4),
                    lhsT_scale=scales[:, P * q : P * (q + 1)],
                    rhs=v_words[:, n // 2, :].bitcast(FP4X4),
                    rhs_scale=v_scales[:, n // 2, :],
                    start=True,
                    stop=True,
                )
                out_banks[s].append(bank)

        def normalise(s):
            n, r0, rows = STEPS[s]
            blocks = rows // P
            q0 = 4 * (n % 2) + r0 // P
            dst = out[n // 2].rearrange("(p q) c -> p q c", q=Q)
            result = work.tile([P, blocks, T], F32, name="result_%d" % blocks, align_bytes=64)
            inverse = []
            for q in range(blocks):
                t = work.tile([P, 1], F32, name="inverse_%d" % q)
                nc.vector.reciprocal(out=t[:], in_=out_banks[s][q][:, T - 1 : T])
                inverse.append(t)
            on_vector = (0, 2, 1, 3)[: OUT_BANKS_ON_VECTOR[s]] if blocks == 4 else range(OUT_BANKS_ON_VECTOR[s])
            for q in range(blocks):
                if q in on_vector:
                    nc.vector.tensor_scalar(
                        out=result[:, q, :], in0=out_banks[s][q][:], scalar1=inverse[q][:], scalar2=None, op0=ALU.mult
                    )
                else:
                    nc.scalar.activation(
                        out=result[:, q, :], in_=out_banks[s][q][:], func=ACT.Copy, scale=inverse[q][:]
                    )
                if s == len(STEPS) - 1:
                    nc.sync.dma_start(out=dst[:, q0 + q : q0 + q + 1, :], in_=result[:, q : q + 1, :])
                elif q % 2:
                    nc.sync.dma_start(out=dst[:, q0 + q - 1 : q0 + q + 1, :], in_=result[:, q - 1 : q + 1, :])

        stages = {
            "p": reorder_x,
            "T": transpose_x,
            "q": quantise_x,
            "a": lambda s: first_matmul(s, (0, 1)),
            "c": lambda s: first_matmul(s, (2, 3)),
            "i": interleave_w,
            "k": quantise_w,
            "B": second_matmul,
            "N": normalise,
            "w": permute_words,
            "s": permute_scales,
        }
        done = {letter: 0 for letter in stages}
        for letter in ORDER:
            stages[letter](done[letter])
            done[letter] += 1
